import numpy as np
import ml_dtypes


def mxq(x, axis, fmt="e4m3"):
    dtype, down = {"e4m3": (ml_dtypes.float8_e4m3fn, 7), "e5m2": (ml_dtypes.float8_e5m2, 14)}[fmt]
    v = np.moveaxis(np.asarray(x, np.float32).astype(ml_dtypes.bfloat16).astype(np.float64), axis, -1)
    blocks = v.reshape(v.shape[:-1] + (-1, 32))
    amax = np.abs(blocks).max(-1, keepdims=True)
    byte = np.maximum(np.where(amax > 0, np.frexp(amax)[1] - 1 + 127, 0) - down, 1)
    scale = np.exp2(byte - 127.0)
    codes = (blocks / scale).astype(np.float32).astype(dtype).astype(np.float64)
    return np.moveaxis((codes * scale).reshape(v.shape), -1, axis)


WIDE = False


def mx_kscale(k):
    if not WIDE:
        return np.ones(k)
    levels = np.array([30, -30])
    if k % 512:
        return np.exp2(np.random.permutation(np.resize(levels, k // 32))).repeat(32)
    a = np.empty((k // 512, 16))
    for p in range(k // 512):
        a[p, :8] = np.random.permutation(np.resize(levels, 8))
        for g in range(8):
            far = levels[np.abs(levels - a[p, g]) >= 10]
            a[p, g + 8] = far[np.random.randint(len(far))]
    return np.exp2(a.ravel()).repeat(32)


def f64(x):
    return np.asarray(x).astype(np.float64)


def striped(idx):
    return np.tile(np.asarray(idx).reshape(-1, 16).T, (8, 1)).astype(np.uint16)


def unstriped(offs):
    return offs[:16].T.reshape(-1).astype(np.int64)


E2M1 = np.array([0.0, 0.5, 1.0, 1.5, 2.0, 3.0, 4.0, 6.0, -0.0, -0.5, -1.0, -1.5, -2.0, -3.0, -4.0, -6.0])


def pack_weight(w, fmt):
    k, n = w.shape
    w = f64(np.asarray(w, np.float32).astype(ml_dtypes.bfloat16)).reshape(k // 32, 32, n)
    amax = np.abs(w).max(1)
    if fmt in ("e4m3", "e5m2"):
        byte = np.frexp(amax)[1] - 1 + 127 - (7 if fmt == "e4m3" else 14)
    else:
        mant, ex = np.frexp(amax / 6.0)
        byte = np.where(mant > 0.5, ex, ex - 1) + 127
    byte = np.clip(np.where(amax > 0, byte, 1), 1, 254)
    scaled = (w * np.exp2(127.0 - byte)[:, None, :]).reshape(k, n).astype(np.float32)
    by_word = np.ascontiguousarray(scaled.reshape(k // 512, 128, 4, n).transpose(0, 1, 3, 2))
    if fmt in ("e4m3", "e5m2"):
        words = by_word.astype(ml_dtypes.float8_e4m3fn if fmt == "e4m3" else ml_dtypes.float8_e5m2).view(np.uint8)
    else:
        c = by_word.astype(ml_dtypes.float4_e2m1fn).view(np.uint8) & 0xF
        words = (c[..., 0::2] | (c[..., 1::2] << 4)).reshape(k // 512, 128, 2 * n)
    return np.ascontiguousarray(words), np.ascontiguousarray(byte.astype(np.uint8).reshape(k // 512, 16, n))


def unpack_weight(words, scales, fmt):
    g, _, n = scales.shape
    words = np.ascontiguousarray(words).reshape(g, 128, n, -1)
    if fmt in ("e4m3", "e5m2"):
        vals = words.view(ml_dtypes.float8_e4m3fn if fmt == "e4m3" else ml_dtypes.float8_e5m2).astype(np.float64)
    else:
        nib = np.empty((g, 128, n, 4), np.uint8)
        nib[..., 0::2] = words & 0xF
        nib[..., 1::2] = words >> 4
        vals = E2M1[nib]
    vals = vals * np.repeat(np.exp2(scales.astype(np.float64) - 127.0), 8, axis=1)[..., None]
    return vals.transpose(0, 1, 3, 2).reshape(g * 512, n)


def sigmoid(v):
    return 1.0 / (1.0 + np.exp(-v))


def sgn(shape):
    return np.random.uniform(0.5, 2.0, shape) * np.where(np.random.standard_normal(shape) < 0, -1.0, 1.0)


K, T, J, R, V, N, O = 512, 1024, 256, 512, 1024, 256, 128


def setup_inputs():
    n = np.random.standard_normal
    idx = np.random.permutation(V)[:R]
    idx2 = np.random.permutation(T)[:J]
    idx3 = np.random.permutation(J)[:O]
    idx4 = np.random.permutation(J)[:O]
    idx5 = np.random.permutation(J)[:O]
    idx6 = np.random.permutation(J)[:O]
    fk = mx_kscale(K)
    fr = mx_kscale(R)
    tr = np.ones(V)
    tr[idx] = fr
    xtp = pack_weight(n((K, T)) / fk[:, None], "e5m2")
    wtp = pack_weight(n((K, V)) * 1 / np.sqrt(K) * fk[:, None] * tr, "e2m1")
    w2p = pack_weight(n((K, R)) * 1 / np.sqrt(K) * fk[:, None] * fr, "e4m3")
    wbp = pack_weight(n((R, N)) * 1 / np.sqrt(R) / fr[:, None], "e2m1")
    wcp = pack_weight(n((R, N)) * 1 / np.sqrt(R) / fr[:, None], "e4m3")
    return {
        "xt_words": xtp[0],
        "xt_scales": xtp[1],
        "wt_words": wtp[0],
        "wt_scales": wtp[1],
        "w2_words": w2p[0],
        "w2_scales": w2p[1],
        "wb_words": wbp[0],
        "wb_scales": wbp[1],
        "wc_words": wcp[0],
        "wc_scales": wcp[1],
        "so": (np.random.uniform(0.5, 1.6, (N, 1))).astype(np.float32),
        "sp": (sgn((N, 1))).astype(np.float32),
        "bo": (np.random.uniform(-2.0, 2.0, (N, 1))).astype(np.float32),
        "so2": (np.random.uniform(0.5, 1.6, (N, 1))).astype(np.float32),
        "sp2": (sgn((N, 1))).astype(np.float32),
        "bo2": (np.random.uniform(-2.0, 2.0, (N, 1))).astype(np.float32),
        "offs": striped(idx),
        "offs2": striped(idx2),
        "offs3": striped(idx3),
        "offs4": striped(idx4),
        "offs5": striped(idx5),
        "offs6": striped(idx6),
    }


def reference(xt_words, xt_scales, wt_words, wt_scales, w2_words, w2_scales, wb_words, wb_scales, wc_words, wc_scales, so, sp, bo, so2, sp2, bo2, offs, offs2, offs3, offs4, offs5, offs6):
    idx = unstriped(offs)
    idx2 = unstriped(offs2)
    idx3 = unstriped(offs3)
    idx4 = unstriped(offs4)
    idx5 = unstriped(offs5)
    idx6 = unstriped(offs6)
    xtu = unpack_weight(xt_words, xt_scales, "e5m2")
    wtu = unpack_weight(wt_words, wt_scales, "e2m1")
    w2u = unpack_weight(w2_words, w2_scales, "e4m3")
    wbu = unpack_weight(wb_words, wb_scales, "e2m1")
    wcu = unpack_weight(wc_words, wc_scales, "e4m3")
    wtidxg = wtu[:, idx]
    xtidx2g = xtu[:, idx2]
    a = wtidxg.T @ xtidx2g
    b = w2u.T @ xtidx2g
    hid = np.abs(a - b)
    hidq = mxq(hid, 0, "e4m3")
    p = wbu.T @ hidq
    q = wcu.T @ hidq
    y = p[:, idx3] * f64(so) * sigmoid(q[:, idx4] * f64(sp) + f64(bo)) - q[:, idx5] * f64(so2) * sigmoid(p[:, idx6] * f64(sp2) + f64(bo2))
    return y

@@ -1,0 +1,222 @@
+from contextlib import ExitStack
+
+import concourse.mybir as mybir
+from concourse.masks import make_identity
+
+K, T, J, R, V, N, O = 512, 1024, 256, 512, 1024, 256, 128
+FLOPS = 2 * (2 * K * R * J + 2 * R * N * J)
+
+F32 = mybir.dt.float32
+BF16 = mybir.dt.bfloat16
+I32 = mybir.dt.int32
+U32 = mybir.dt.uint32
+U16 = mybir.dt.uint16
+U8 = mybir.dt.uint8
+E4M3 = mybir.dt.float8_e4m3fn_x4
+E5M2 = mybir.dt.float8_e5m2_x4
+E2M1 = mybir.dt.float4_e2m1fn_x4
+ACT = mybir.ActivationFunctionType
+ALU = mybir.AluOpType
+
+P = 128
+PACK = 4
+LANES = 16
+R_PIECES = ((0, 256), (256, 384), (384, 512))
+
+
+def tile_list_outcomegatedcross_storeleads_kernel(
+    tc, xt_words, xt_scales, wt_words, wt_scales, w2_words, w2_scales, wb_words, wb_scales, wc_words, wc_scales,
+    so, sp, bo, so2, sp2, bo2, offs, offs2, offs3, offs4, offs5, offs6, out,
+):
+    nc = tc.nc
+    halves = range(2)
+
+    with ExitStack() as ctx:
+        sb = ctx.enter_context(tc.tile_pool(name="sb", bufs=1))
+        ps = ctx.enter_context(tc.psum_pool(name="ps", bufs=1))
+
+        def tile(name, shape, dtype, tag=None):
+            return sb.tile(shape, dtype, name=name, tag=name if tag is None else tag, align_bytes=64)
+
+        def bank(name, tag, shape):
+            return ps.tile(shape, F32, name=name, tag=tag)
+
+        def load_list(name, src):
+            dst = tile(name, list(src.shape), U16)
+            nc.sync.dma_start(dst[:], src)
+            return dst
+
+        def load_words(queue, dst, src):
+            queue.dma_start(dst[:].bitcast(I32), src.bitcast(I32))
+
+        def load_scale_rows(queue, plane, src, quadrant):
+            queue.dma_start(
+                plane[32 * quadrant : 32 * quadrant + 4, :].bitcast(I32),
+                src[0, 4 * quadrant : 4 * quadrant + 4, :].bitcast(I32),
+            )
+
+        def load_folded(folded, src, first=0):
+            cols = slice(first // 4, (first + src.shape[2]) // 4)
+            rows = src[0].rearrange("(a b r) c -> b r a c", a=2, b=2)
+            for b in halves:
+                nc.sync.dma_start(
+                    folded[32 * b : 32 * b + 4, :].bitcast(I32).rearrange("r (a c) -> r a c", a=2)[:, :, cols],
+                    rows[b].bitcast(I32)
+                )
+
+        def unfold(plane, folded, a):
+            width = folded.shape[1] // 2
+            nc.vector.tensor_copy(
+                plane[64 * a : 64 * (a + 1), 0:width].bitcast(I32), folded[0:64, a * width : (a + 1) * width].bitcast(I32)
+            )
+
+        def load_columns(name, src):
+            dst = tile(name, [P, 2], F32)
+            with nc.allow_non_contiguous_dma(reason="one value for each partition"):
+                nc.sync.dma_start(dst[:], src.rearrange("(h p) one -> p (h one)", p=P))
+            return dst
+
+        xt_w = tile("xt_w", [P, T], U32)
+        xt_s = tile("xt_s", [P, T], U8)
+        wt_w = tile("wt_w", [P, V], U16)
+        wt_s = tile("wt_s", [P, V], U8)
+        w2_w = tile("w2_w", [P, R], U32)
+        w2_s = tile("w2_s", [P, 2 * R], U8)
+        wb_w = tile("wb_w", [P, 2 * N], U8)
+        wc_w = tile("wc_w", [P, N], U32)
+        out_folded = tile("out_folded", [P, 4 * N], U8)
+        identity = tile("identity", [P, P], F32)
+
+        nc.vector.memset(xt_s[:].bitcast(I32), 0)
+        for plane in (w2_s, wt_s, out_folded):
+            nc.gpsimd.memset(plane[:].bitcast(I32), 0)
+
+        load_words(nc.sync, wt_w, wt_words[0])
+        store_list = load_list("store_list", offs)
+        token_list = load_list("token_list", offs2)
+        for quadrant, queue in enumerate((nc.scalar, nc.scalar, nc.sync, nc.sync)):
+            load_scale_rows(queue, xt_s, xt_scales, quadrant)
+        load_words(nc.sync, xt_w, xt_words[0].rearrange("p c t -> p (c t)"))
+        load_folded(w2_s, w2_scales)
+        unfold(w2_s, w2_s, 1)
+        load_words(nc.sync, w2_w, w2_words[0].rearrange("p c t -> p (c t)"))
+        for quadrant in range(4):
+            load_scale_rows(nc.sync, wt_s, wt_scales, quadrant)
+        load_folded(out_folded, wb_scales)
+        load_folded(out_folded, wc_scales, N)
+        load_words(nc.sync, wb_w, wb_words[0])
+        load_words(nc.sync, wc_w, wc_words[0].rearrange("p c t -> p (c t)"))
+        p_gate_list = load_list("p_gate_list", offs6)
+        p_gate_slope = load_columns("p_gate_slope", sp2)
+        p_gate_offset = load_columns("p_gate_offset", bo2)
+        p_list = load_list("p_list", offs3)
+        p_weight = load_columns("p_weight", so)
+        q_gate_list = load_list("q_gate_list", offs4)
+        q_gate_slope = load_columns("q_gate_slope", sp)
+        q_gate_offset = load_columns("q_gate_offset", bo)
+        q_list = load_list("q_list", offs5)
+        q_weight = load_columns("q_weight", so2)
+
+        make_identity(nc, identity[:])
+
+        wg_w = tile("wg_w", [P, R], U16)
+        xg_s = tile("xg_s", [P, J], U8)
+        xg_w = tile("xg_w", [P, J], U32)
+        nc.vector.tensor_copy(wg_w[:], wt_w[:].indirect(store_list[:]))
+        nc.vector.tensor_copy(xg_s[:], xt_s[:].indirect(token_list[:]))
+        nc.vector.tensor_copy(xg_w[:], xt_w[:].indirect(token_list[:]))
+        wg_s = []
+        for piece, (first, last) in enumerate(R_PIECES):
+            scales = tile("wg_s%d" % piece, [P, last - first], U8)
+            nc.vector.tensor_copy(scales[:], wt_s[:].indirect(store_list[:, first // LANES : last // LANES]))
+            wg_s.append(scales)
+
+        def times_tokens(dst, jt, words, scales):
+            slots = slice(jt * P, (jt + 1) * P)
+            nc.tensor.matmul_mx(
+                out=dst, lhsT=xg_w[:, slots].bitcast(E5M2), lhsT_scale=xg_s[:, slots],
+                rhs=words, rhs_scale=scales, start=True, stop=True,
+            )
+
+        b_sb = []
+        for jt in halves:
+            b_ps = bank("b_ps%d" % jt, "b%d" % jt, [P, R])
+            times_tokens(b_ps[:], jt, w2_w[:].bitcast(E4M3), w2_s[:, 0:R])
+            b_dealt = tile("b_sb%d" % jt, [P, PACK, P], F32)
+            nc.scalar.copy(b_dealt[:], b_ps[:].rearrange("j (p t) -> j t p", t=PACK))
+            b_sb.append(b_dealt)
+
+        a_first = [bank("a_first%d" % i, "a%d" % i, [P, last - first]) for i, (first, last) in enumerate(R_PIECES)]
+        a_second = bank("a_second", "a3", [P, R])
+        for jt in halves:
+            for piece, (first, last) in enumerate(R_PIECES):
+                dst = a_first[piece][:] if jt == 0 else a_second[:, first:last]
+                times_tokens(dst, jt, wg_w[:, first:last].bitcast(E2M1), wg_s[piece][:])
+
+        turned = []
+        for jt, parts in enumerate((list(zip(a_first, R_PIECES)), [(a_second, (0, R))])):
+            diff = tile("diff%d" % jt, [P, PACK, P], F32)
+            for a_ps, (first, last) in parts:
+                rows = slice(first // PACK, last // PACK)
+                nc.vector.tensor_tensor(
+                    diff[:, :, rows], a_ps[:].rearrange("j (p t) -> j t p", t=PACK), b_sb[jt][:, :, rows], ALU.subtract
+                )
+            diff_ps = bank("diff_ps%d" % jt, "b%d" % jt, [P, PACK, P])
+            for t in range(PACK):
+                nc.tensor.transpose(diff_ps[:, t, :], diff[:, t, :], identity[:])
+            turned.append(diff_ps)
+
+        out_s = tile("out_s", [P, 2 * N], U8, tag="b_sb1")
+        for a in halves:
+            unfold(out_s, out_folded, a)
+
+        outcome = {(m, h): tile("%s%d" % (m, h), [P, J], F32) for m in "pq" for h in halves}
+        weights = {"p": (wb_w, out_s[:, 0:N], E2M1, 2), "q": (wc_w, out_s[:, N : 2 * N], E4M3, 1)}
+        lead, *rest = outcome
+        lead_ps = [bank("lead_ps%d" % jt, "lead%d" % jt, [P, P]) for jt in halves]
+        rest_ps = {key: bank("rest_ps%d" % i, "a%d" % i, [P, J]) for i, key in enumerate(rest)}
+        for jt in halves:
+            slots = slice(jt * P, (jt + 1) * P)
+            hid = tile("hid%d" % jt, [P, P, PACK], BF16)
+            nc.scalar.activation(hid[:], turned[jt][:].rearrange("p t j -> p j t"), ACT.Abs)
+            hid_w = tile("hid_w%d" % jt, [P, P], U32)
+            hid_s = tile("hid_s%d" % jt, [P, P], U8)
+            nc.vector.quantize_mx(hid_w[:].bitcast(E4M3), hid_s[:], hid[:].rearrange("p j t -> p (j t)"))
+            for m, h in outcome:
+                words, scales, fmt, width = weights[m]
+                nc.tensor.matmul_mx(
+                    out=lead_ps[jt][:] if (m, h) == lead else rest_ps[m, h][:, slots],
+                    lhsT=words[:, width * h * P : width * (h + 1) * P].bitcast(fmt),
+                    lhsT_scale=scales[:, h * P : (h + 1) * P],
+                    rhs=hid_w[:].bitcast(E4M3), rhs_scale=hid_s[:], start=True, stop=True,
+                )
+            nc.vector.tensor_copy(outcome[lead][:, slots], lead_ps[jt][:])
+        for key in rest:
+            nc.vector.tensor_copy(outcome[key][:], rest_ps[key][:])
+
+        def look(name, m, entries, func, **affine):
+            picked = []
+            for h in halves:
+                dst = tile("%s%d" % (name, h), [P, O], F32)
+                columns = {key: vector[:, h : h + 1] for key, vector in affine.items()}
+                nc.scalar.activation(dst[:], outcome[m, h][:].indirect(entries[:]), func, **columns)
+                picked.append(dst)
+            return picked
+
+        def combine(name, left, right, op):
+            made = []
+            for h in halves:
+                dst = tile("%s%d" % (name, h), [P, O], F32)
+                nc.vector.tensor_tensor(dst[:], left[h][:], right[h][:], op)
+                made.append(dst)
+            return made
+
+        p_gate = look("p_gate", "p", p_gate_list, ACT.Sigmoid, scale=p_gate_slope, bias=p_gate_offset)
+        p_term = look("p_term", "p", p_list, ACT.Copy, scale=p_weight)
+        q_gate = look("q_gate", "q", q_gate_list, ACT.Sigmoid, scale=q_gate_slope, bias=q_gate_offset)
+        first = combine("first", p_term, q_gate, ALU.mult)
+        q_term = look("q_term", "q", q_list, ACT.Copy, scale=q_weight)
+        second = combine("second", q_term, p_gate, ALU.mult)
+        result = combine("result", first, second, ALU.subtract)
+        for h in halves:
+            nc.sync.dma_start(out[h * P : (h + 1) * P, :], result[h][:])

@@ -55,11 +55,11 @@ def tile_list_outcomegatedcross_storeleads_kernel(
                 src[0, 4 * quadrant : 4 * quadrant + 4, :].bitcast(I32),
             )
 
-        def load_folded(folded, src, first=0):
+        def load_folded(queue, folded, src, first=0):
             cols = slice(first // 4, (first + src.shape[2]) // 4)
             rows = src[0].rearrange("(a b r) c -> b r a c", a=2, b=2)
             for b in halves:
-                nc.sync.dma_start(
+                queue.dma_start(
                     folded[32 * b : 32 * b + 4, :].bitcast(I32).rearrange("r (a c) -> r a c", a=2)[:, :, cols],
                     rows[b].bitcast(I32)
                 )
@@ -90,6 +90,7 @@ def tile_list_outcomegatedcross_storeleads_kernel(
         nc.vector.memset(xt_s[:].bitcast(I32), 0)
         for plane in (w2_s, wt_s, out_folded):
             nc.gpsimd.memset(plane[:].bitcast(I32), 0)
+        make_identity(nc, identity[:])
 
         load_words(nc.sync, wt_w, wt_words[0])
         store_list = load_list("store_list", offs)
@@ -97,13 +98,13 @@ def tile_list_outcomegatedcross_storeleads_kernel(
         for quadrant, queue in enumerate((nc.scalar, nc.scalar, nc.sync, nc.sync)):
             load_scale_rows(queue, xt_s, xt_scales, quadrant)
         load_words(nc.sync, xt_w, xt_words[0].rearrange("p c t -> p (c t)"))
-        load_folded(w2_s, w2_scales)
-        unfold(w2_s, w2_s, 1)
         load_words(nc.sync, w2_w, w2_words[0].rearrange("p c t -> p (c t)"))
+        load_folded(nc.sync, w2_s, w2_scales)
+        unfold(w2_s, w2_s, 1)
         for quadrant in range(4):
             load_scale_rows(nc.sync, wt_s, wt_scales, quadrant)
-        load_folded(out_folded, wb_scales)
-        load_folded(out_folded, wc_scales, N)
+        load_folded(nc.sync, out_folded, wb_scales)
+        load_folded(nc.sync, out_folded, wc_scales, N)
         load_words(nc.sync, wb_w, wb_words[0])
         load_words(nc.sync, wc_w, wc_words[0].rearrange("p c t -> p (c t)"))
         p_gate_list = load_list("p_gate_list", offs6)
@@ -117,7 +118,10 @@ def tile_list_outcomegatedcross_storeleads_kernel(
         q_list = load_list("q_list", offs5)
         q_weight = load_columns("q_weight", so2)
 
-        make_identity(nc, identity[:])
+        warm_in = tile("warm_in", [P, 1], F32)
+        warm_out = tile("warm_out", [P, 1], F32)
+        nc.vector.memset(warm_in[:], 0.0)
+        nc.scalar.activation(warm_out[:], warm_in[:], ACT.Sigmoid)
 
         wg_w = tile("wg_w", [P, R], U16)
         xg_s = tile("xg_s", [P, J], U8)
@@ -146,20 +150,20 @@ def tile_list_outcomegatedcross_storeleads_kernel(
             nc.scalar.copy(b_dealt[:], b_ps[:].rearrange("j (p t) -> j t p", t=PACK))
             b_sb.append(b_dealt)
 
-        a_first = [bank("a_first%d" % i, "a%d" % i, [P, last - first]) for i, (first, last) in enumerate(R_PIECES)]
-        a_second = bank("a_second", "a3", [P, R])
-        for jt in halves:
-            for piece, (first, last) in enumerate(R_PIECES):
-                dst = a_first[piece][:] if jt == 0 else a_second[:, first:last]
-                times_tokens(dst, jt, wg_w[:, first:last].bitcast(E2M1), wg_s[piece][:])
+        a_ps = {}
+        for piece, jt in ((0, 0), (0, 1), (1, 0), (2, 0), (1, 1), (2, 1)):
+            first, last = R_PIECES[piece]
+            a_ps[jt, piece] = bank("a_ps%d%d" % (jt, piece), "a%d%d" % (jt, piece), [P, last - first])
+            times_tokens(a_ps[jt, piece][:], jt, wg_w[:, first:last].bitcast(E2M1), wg_s[piece][:])
 
         turned = []
-        for jt, parts in enumerate((list(zip(a_first, R_PIECES)), [(a_second, (0, R))])):
+        for jt in halves:
             diff = tile("diff%d" % jt, [P, PACK, P], F32)
-            for a_ps, (first, last) in parts:
+            for piece, (first, last) in enumerate(R_PIECES):
                 rows = slice(first // PACK, last // PACK)
                 nc.vector.tensor_tensor(
-                    diff[:, :, rows], a_ps[:].rearrange("j (p t) -> j t p", t=PACK), b_sb[jt][:, :, rows], ALU.subtract
+                    diff[:, :, rows], a_ps[jt, piece][:].rearrange("j (p t) -> j t p", t=PACK), b_sb[jt][:, :, rows],
+                    ALU.subtract,
                 )
             diff_ps = bank("diff_ps%d" % jt, "b%d" % jt, [P, PACK, P])
             for t in range(PACK):
@@ -172,11 +176,8 @@ def tile_list_outcomegatedcross_storeleads_kernel(
 
         outcome = {(m, h): tile("%s%d" % (m, h), [P, J], F32) for m in "pq" for h in halves}
         weights = {"p": (wb_w, out_s[:, 0:N], E2M1, 2), "q": (wc_w, out_s[:, N : 2 * N], E4M3, 1)}
-        lead, *rest = outcome
-        lead_ps = [bank("lead_ps%d" % jt, "lead%d" % jt, [P, P]) for jt in halves]
-        rest_ps = {key: bank("rest_ps%d" % i, "a%d" % i, [P, J]) for i, key in enumerate(rest)}
+        sums = {key: bank("sums_" + tag, tag, [P, J]) for key, tag in zip(outcome, ("a00", "a01", "a02", "a10"))}
         for jt in halves:
-            slots = slice(jt * P, (jt + 1) * P)
             hid = tile("hid%d" % jt, [P, P, PACK], BF16)
             nc.scalar.activation(hid[:], turned[jt][:].rearrange("p t j -> p j t"), ACT.Abs)
             hid_w = tile("hid_w%d" % jt, [P, P], U32)
@@ -185,14 +186,13 @@ def tile_list_outcomegatedcross_storeleads_kernel(
             for m, h in outcome:
                 words, scales, fmt, width = weights[m]
                 nc.tensor.matmul_mx(
-                    out=lead_ps[jt][:] if (m, h) == lead else rest_ps[m, h][:, slots],
+                    out=sums[m, h][:, jt * P : (jt + 1) * P],
                     lhsT=words[:, width * h * P : width * (h + 1) * P].bitcast(fmt),
                     lhsT_scale=scales[:, h * P : (h + 1) * P],
                     rhs=hid_w[:].bitcast(E4M3), rhs_scale=hid_s[:], start=True, stop=True,
                 )
-            nc.vector.tensor_copy(outcome[lead][:, slots], lead_ps[jt][:])
-        for key in rest:
-            nc.vector.tensor_copy(outcome[key][:], rest_ps[key][:])
+        for key in outcome:
+            nc.vector.tensor_copy(outcome[key][:], sums[key][:])
 
         def look(name, m, entries, func, **affine):
             picked = []

from contextlib import ExitStack

import concourse.mybir as mybir
from concourse.masks import make_identity

K, T, J, R, V, N, O = 512, 1024, 256, 512, 1024, 256, 128
FLOPS = 2 * (2 * K * R * J + 2 * R * N * J)

F32 = mybir.dt.float32
BF16 = mybir.dt.bfloat16
I32 = mybir.dt.int32
U32 = mybir.dt.uint32
U16 = mybir.dt.uint16
U8 = mybir.dt.uint8
E4M3 = mybir.dt.float8_e4m3fn_x4
E5M2 = mybir.dt.float8_e5m2_x4
E2M1 = mybir.dt.float4_e2m1fn_x4
ACT = mybir.ActivationFunctionType
ALU = mybir.AluOpType

P = 128
PACK = 4
LANES = 16
R_PIECES = ((0, 256), (256, 384), (384, 512))


def tile_list_outcomegatedcross_storeleads_kernel(
    tc, xt_words, xt_scales, wt_words, wt_scales, w2_words, w2_scales, wb_words, wb_scales, wc_words, wc_scales,
    so, sp, bo, so2, sp2, bo2, offs, offs2, offs3, offs4, offs5, offs6, out,
):
    nc = tc.nc
    halves = range(2)

    with ExitStack() as ctx:
        sb = ctx.enter_context(tc.tile_pool(name="sb", bufs=1))
        ps = ctx.enter_context(tc.psum_pool(name="ps", bufs=1))

        def tile(name, shape, dtype, tag=None):
            return sb.tile(shape, dtype, name=name, tag=name if tag is None else tag, align_bytes=64)

        def bank(name, tag, shape):
            return ps.tile(shape, F32, name=name, tag=tag)

        def load_list(name, src):
            dst = tile(name, list(src.shape), U16)
            nc.sync.dma_start(dst[:], src)
            return dst

        def load_words(queue, dst, src):
            queue.dma_start(dst[:].bitcast(I32), src.bitcast(I32))

        def load_scale_rows(queue, plane, src, quadrant):
            queue.dma_start(
                plane[32 * quadrant : 32 * quadrant + 4, :].bitcast(I32),
                src[0, 4 * quadrant : 4 * quadrant + 4, :].bitcast(I32),
            )

        def load_folded(queue, folded, src, first=0):
            cols = slice(first // 4, (first + src.shape[2]) // 4)
            rows = src[0].rearrange("(a b r) c -> b r a c", a=2, b=2)
            for b in halves:
                queue.dma_start(
                    folded[32 * b : 32 * b + 4, :].bitcast(I32).rearrange("r (a c) -> r a c", a=2)[:, :, cols],
                    rows[b].bitcast(I32)
                )

        def unfold(plane, folded, a):
            width = folded.shape[1] // 2
            nc.vector.tensor_copy(
                plane[64 * a : 64 * (a + 1), 0:width].bitcast(I32), folded[0:64, a * width : (a + 1) * width].bitcast(I32)
            )

        def load_columns(name, src):
            dst = tile(name, [P, 2], F32)
            with nc.allow_non_contiguous_dma(reason="one value for each partition"):
                nc.sync.dma_start(dst[:], src.rearrange("(h p) one -> p (h one)", p=P))
            return dst

        xt_w = tile("xt_w", [P, T], U32)
        xt_s = tile("xt_s", [P, T], U8)
        wt_w = tile("wt_w", [P, V], U16)
        wt_s = tile("wt_s", [P, V], U8)
        w2_w = tile("w2_w", [P, R], U32)
        w2_s = tile("w2_s", [P, 2 * R], U8)
        wb_w = tile("wb_w", [P, 2 * N], U8)
        wc_w = tile("wc_w", [P, N], U32)
        out_folded = tile("out_folded", [P, 4 * N], U8)
        identity = tile("identity", [P, P], F32)

        nc.vector.memset(xt_s[:].bitcast(I32), 0)
        for plane in (w2_s, wt_s, out_folded):
            nc.gpsimd.memset(plane[:].bitcast(I32), 0)
        make_identity(nc, identity[:])

        load_words(nc.sync, wt_w, wt_words[0])
        store_list = load_list("store_list", offs)
        token_list = load_list("token_list", offs2)
        for quadrant, queue in enumerate((nc.scalar, nc.scalar, nc.sync, nc.sync)):
            load_scale_rows(queue, xt_s, xt_scales, quadrant)
        load_words(nc.sync, xt_w, xt_words[0].rearrange("p c t -> p (c t)"))
        load_words(nc.sync, w2_w, w2_words[0].rearrange("p c t -> p (c t)"))
        load_folded(nc.sync, w2_s, w2_scales)
        unfold(w2_s, w2_s, 1)
        for quadrant in range(4):
            load_scale_rows(nc.sync, wt_s, wt_scales, quadrant)
        load_folded(nc.sync, out_folded, wb_scales)
        load_folded(nc.sync, out_folded, wc_scales, N)
        load_words(nc.sync, wb_w, wb_words[0])
        load_words(nc.sync, wc_w, wc_words[0].rearrange("p c t -> p (c t)"))
        p_gate_list = load_list("p_gate_list", offs6)
        p_gate_slope = load_columns("p_gate_slope", sp2)
        p_gate_offset = load_columns("p_gate_offset", bo2)
        p_list = load_list("p_list", offs3)
        p_weight = load_columns("p_weight", so)
        q_gate_list = load_list("q_gate_list", offs4)
        q_gate_slope = load_columns("q_gate_slope", sp)
        q_gate_offset = load_columns("q_gate_offset", bo)
        q_list = load_list("q_list", offs5)
        q_weight = load_columns("q_weight", so2)

        warm_in = tile("warm_in", [P, 1], F32)
        warm_out = tile("warm_out", [P, 1], F32)
        nc.vector.memset(warm_in[:], 0.0)
        nc.scalar.activation(warm_out[:], warm_in[:], ACT.Sigmoid)

        wg_w = tile("wg_w", [P, R], U16)
        xg_s = tile("xg_s", [P, J], U8)
        xg_w = tile("xg_w", [P, J], U32)
        nc.vector.tensor_copy(wg_w[:], wt_w[:].indirect(store_list[:]))
        nc.vector.tensor_copy(xg_s[:], xt_s[:].indirect(token_list[:]))
        nc.vector.tensor_copy(xg_w[:], xt_w[:].indirect(token_list[:]))
        wg_s = []
        for piece, (first, last) in enumerate(R_PIECES):
            scales = tile("wg_s%d" % piece, [P, last - first], U8)
            nc.vector.tensor_copy(scales[:], wt_s[:].indirect(store_list[:, first // LANES : last // LANES]))
            wg_s.append(scales)

        def times_tokens(dst, jt, words, scales):
            slots = slice(jt * P, (jt + 1) * P)
            nc.tensor.matmul_mx(
                out=dst, lhsT=xg_w[:, slots].bitcast(E5M2), lhsT_scale=xg_s[:, slots],
                rhs=words, rhs_scale=scales, start=True, stop=True,
            )

        b_sb = []
        for jt in halves:
            b_ps = bank("b_ps%d" % jt, "b%d" % jt, [P, R])
            times_tokens(b_ps[:], jt, w2_w[:].bitcast(E4M3), w2_s[:, 0:R])
            b_dealt = tile("b_sb%d" % jt, [P, PACK, P], F32)
            nc.scalar.copy(b_dealt[:], b_ps[:].rearrange("j (p t) -> j t p", t=PACK))
            b_sb.append(b_dealt)

        a_ps = {}
        for piece, jt in ((0, 0), (0, 1), (1, 0), (2, 0), (1, 1), (2, 1)):
            first, last = R_PIECES[piece]
            a_ps[jt, piece] = bank("a_ps%d%d" % (jt, piece), "a%d%d" % (jt, piece), [P, last - first])
            times_tokens(a_ps[jt, piece][:], jt, wg_w[:, first:last].bitcast(E2M1), wg_s[piece][:])

        turned = []
        for jt in halves:
            diff = tile("diff%d" % jt, [P, PACK, P], F32)
            for piece, (first, last) in enumerate(R_PIECES):
                rows = slice(first // PACK, last // PACK)
                nc.vector.tensor_tensor(
                    diff[:, :, rows], a_ps[jt, piece][:].rearrange("j (p t) -> j t p", t=PACK), b_sb[jt][:, :, rows],
                    ALU.subtract,
                )
            diff_ps = bank("diff_ps%d" % jt, "b%d" % jt, [P, PACK, P])
            for t in range(PACK):
                nc.tensor.transpose(diff_ps[:, t, :], diff[:, t, :], identity[:])
            turned.append(diff_ps)

        out_s = tile("out_s", [P, 2 * N], U8, tag="b_sb1")
        for a in halves:
            unfold(out_s, out_folded, a)

        outcome = {(m, h): tile("%s%d" % (m, h), [P, J], F32) for m in "pq" for h in halves}
        weights = {"p": (wb_w, out_s[:, 0:N], E2M1, 2), "q": (wc_w, out_s[:, N : 2 * N], E4M3, 1)}
        sums = {key: bank("sums_" + tag, tag, [P, J]) for key, tag in zip(outcome, ("a00", "a01", "a02", "a10"))}
        for jt in halves:
            hid = tile("hid%d" % jt, [P, P, PACK], BF16)
            nc.scalar.activation(hid[:], turned[jt][:].rearrange("p t j -> p j t"), ACT.Abs)
            hid_w = tile("hid_w%d" % jt, [P, P], U32)
            hid_s = tile("hid_s%d" % jt, [P, P], U8)
            nc.vector.quantize_mx(hid_w[:].bitcast(E4M3), hid_s[:], hid[:].rearrange("p j t -> p (j t)"))
            for m, h in outcome:
                words, scales, fmt, width = weights[m]
                nc.tensor.matmul_mx(
                    out=sums[m, h][:, jt * P : (jt + 1) * P],
                    lhsT=words[:, width * h * P : width * (h + 1) * P].bitcast(fmt),
                    lhsT_scale=scales[:, h * P : (h + 1) * P],
                    rhs=hid_w[:].bitcast(E4M3), rhs_scale=hid_s[:], start=True, stop=True,
                )
        for key in outcome:
            nc.vector.tensor_copy(outcome[key][:], sums[key][:])

        def look(name, m, entries, func, **affine):
            picked = []
            for h in halves:
                dst = tile("%s%d" % (name, h), [P, O], F32)
                columns = {key: vector[:, h : h + 1] for key, vector in affine.items()}
                nc.scalar.activation(dst[:], outcome[m, h][:].indirect(entries[:]), func, **columns)
                picked.append(dst)
            return picked

        def combine(name, left, right, op):
            made = []
            for h in halves:
                dst = tile("%s%d" % (name, h), [P, O], F32)
                nc.vector.tensor_tensor(dst[:], left[h][:], right[h][:], op)
                made.append(dst)
            return made

        p_gate = look("p_gate", "p", p_gate_list, ACT.Sigmoid, scale=p_gate_slope, bias=p_gate_offset)
        p_term = look("p_term", "p", p_list, ACT.Copy, scale=p_weight)
        q_gate = look("q_gate", "q", q_gate_list, ACT.Sigmoid, scale=q_gate_slope, bias=q_gate_offset)
        first = combine("first", p_term, q_gate, ALU.mult)
        q_term = look("q_term", "q", q_list, ACT.Copy, scale=q_weight)
        second = combine("second", q_term, p_gate, ALU.mult)
        result = combine("result", first, second, ALU.subtract)
        for h in halves:
            nc.sync.dma_start(out[h * P : (h + 1) * P, :], result[h][:])
